import numpy as np
import ml_dtypes


def mxq(x, axis, fmt="e4m3"):
    dtype, down = {"e4m3": (ml_dtypes.float8_e4m3fn, 7), "e5m2": (ml_dtypes.float8_e5m2, 14)}[fmt]
    v = np.moveaxis(np.asarray(x, np.float32).astype(ml_dtypes.bfloat16).astype(np.float64), axis, -1)
    blocks = v.reshape(v.shape[:-1] + (-1, 32))
    amax = np.abs(blocks).max(-1, keepdims=True)
    byte = np.maximum(np.where(amax > 0, np.frexp(amax)[1] - 1 + 127, 0) - down, 1)
    scale = np.exp2(byte - 127.0)
    codes = (blocks / scale).astype(np.float32).astype(dtype).astype(np.float64)
    return np.moveaxis((codes * scale).reshape(v.shape), -1, axis)


WIDE = False


def mx_kscale(k):
    if not WIDE:
        return np.ones(k)
    levels = np.array([10, -10, 5, -5, 0])
    if k % 512:
        return np.exp2(np.random.permutation(np.resize(levels, k // 32))).repeat(32)
    a = np.empty((k // 512, 16))
    for p in range(k // 512):
        a[p, :8] = np.random.permutation(np.resize(levels, 8))
        for g in range(8):
            far = levels[np.abs(levels - a[p, g]) >= 10]
            a[p, g + 8] = far[np.random.randint(len(far))]
    return np.exp2(a.ravel()).repeat(32)


def f64(x):
    return np.asarray(x).astype(np.float64)


def striped(idx):
    return np.tile(np.asarray(idx).reshape(-1, 16).T, (8, 1)).astype(np.uint16)


def unstriped(offs):
    return offs[:16].T.reshape(-1).astype(np.int64)


def striped8(idx):
    return np.asarray(idx).reshape(8, -1, 16).transpose(0, 2, 1).reshape(128, -1).astype(np.uint16)


def unstriped8(offs):
    return offs.reshape(8, 16, -1).transpose(0, 2, 1).reshape(8, -1).astype(np.int64)


def pick8(x, idx, run):
    r = np.arange(len(x))
    return x[r[:, None], idx[r % (8 * run) // run]]


E2M1 = np.array([0.0, 0.5, 1.0, 1.5, 2.0, 3.0, 4.0, 6.0, -0.0, -0.5, -1.0, -1.5, -2.0, -3.0, -4.0, -6.0])


def pack_weight(w, fmt):
    k, n = w.shape
    w = f64(np.asarray(w, np.float32).astype(ml_dtypes.bfloat16)).reshape(k // 32, 32, n)
    amax = np.abs(w).max(1)
    if fmt == "e4m3":
        byte = np.frexp(amax)[1] - 1 + 127 - 7
    else:
        mant, ex = np.frexp(amax / 6.0)
        byte = np.where(mant > 0.5, ex, ex - 1) + 127
    byte = np.clip(np.where(amax > 0, byte, 1), 1, 254)
    scaled = (w * np.exp2(127.0 - byte)[:, None, :]).reshape(k, n).astype(np.float32)
    by_word = np.ascontiguousarray(scaled.reshape(k // 512, 128, 4, n).transpose(0, 1, 3, 2))
    if fmt == "e4m3":
        words = by_word.astype(ml_dtypes.float8_e4m3fn).view(np.uint8)
    else:
        c = by_word.astype(ml_dtypes.float4_e2m1fn).view(np.uint8) & 0xF
        words = (c[..., 0::2] | (c[..., 1::2] << 4)).reshape(k // 512, 128, 2 * n)
    return np.ascontiguousarray(words), np.ascontiguousarray(byte.astype(np.uint8).reshape(k // 512, 16, n))


def unpack_weight(words, scales, fmt):
    g, _, n = scales.shape
    words = np.ascontiguousarray(words).reshape(g, 128, n, -1)
    if fmt == "e4m3":
        vals = words.view(ml_dtypes.float8_e4m3fn).astype(np.float64)
    else:
        nib = np.empty((g, 128, n, 4), np.uint8)
        nib[..., 0::2] = words & 0xF
        nib[..., 1::2] = words >> 4
        vals = E2M1[nib]
    vals = vals * np.repeat(np.exp2(scales.astype(np.float64) - 127.0), 8, axis=1)[..., None]
    return vals.transpose(0, 1, 3, 2).reshape(g * 512, n)


K, J, R, T, F, C, O, N, S, Z = 512, 256, 512, 1024, 1024, 512, 128, 256, 1024, 512


def setup_inputs():
    n = np.random.standard_normal
    idx = np.random.permutation(T)[:J]
    idx2 = np.stack([np.random.permutation(F)[:R] for _ in range(8)])
    idx3 = np.random.permutation(C)[:J]
    idx4 = np.random.permutation(C)[:O]
    idx5 = np.stack([np.random.permutation(C)[:O] for _ in range(8)])
    idx6 = np.stack([np.random.permutation(S)[:Z] for _ in range(8)])
    idx7 = np.random.permutation(Z)[:N]
    fk = mx_kscale(K)
    fr = mx_kscale(R)
    xtp = pack_weight(n((K, T)) * fk[:, None], "e2m1")
    return {
        "xt_words": xtp[0],
        "xt_scales": xtp[1],
        "ua": (np.random.randint(-7, 8, (K, F)).astype(np.float64)).astype(np.float32),
        "ha": ((np.random.randint(8, 25, (K, 1)) / 1024.0) / fk[:, None]).astype(np.float32),
        "sa": (np.random.uniform(0.5, 1.6, (R, 1)) * fr[:, None]).astype(np.float32),
        "sb": (np.random.uniform(0.5, 1.6, (R, 1)) * fr[:, None]).astype(np.float32),
        "va": (np.random.randint(-7, 8, (R, S)).astype(np.float64)).astype(np.float32),
        "ea": ((np.random.randint(8, 25, (R, 1)) / 1024.0) / fr[:, None]).astype(np.float32),
        "eb": (np.random.uniform(0.5, 1.6, (R, 1))).astype(np.float32),
        "offs": striped(idx),
        "offs2": striped8(idx2),
        "offs3": striped(idx3),
        "offs4": striped(idx4),
        "offs5": striped8(idx5),
        "offs6": striped8(idx6),
        "offs7": striped(idx7),
    }


def reference(xt_words, xt_scales, ua, ha, sa, sb, va, ea, eb, offs, offs2, offs3, offs4, offs5, offs6, offs7):
    idx = unstriped(offs)
    idx2 = unstriped8(offs2)
    idx3 = unstriped(offs3)
    idx4 = unstriped(offs4)
    idx5 = unstriped8(offs5)
    idx6 = unstriped8(offs6)
    idx7 = unstriped(offs7)
    xtu = unpack_weight(xt_words, xt_scales, "e2m1")
    wc = pick8(f64(ua), idx2, 64) * f64(ha)
    wcq = mxq(wc, 0, "e4m3")
    xtidxg = xtu[:, idx]
    a = wcq.T @ xtidxg
    pw = np.zeros((R, C))
    pw[:, idx3] = a
    hid = np.abs(pw[:, idx4] * f64(sa) - pick8(pw, idx5, 64) * f64(sb))
    vcd = pick8(f64(va), idx6, 64) * f64(ea)
    vc = vcd[:, idx7] * f64(eb)
    vcq = mxq(vc, 0, "e4m3")
    hidq = mxq(hid, 0, "e4m3")
    y = vcq.T @ hidq
    return y

@@ -1,0 +1,179 @@
+from contextlib import ExitStack
+
+import concourse.mybir as mybir
+
+K, J, R, T, F, C, O, N, S, Z = 512, 256, 512, 1024, 1024, 512, 128, 256, 1024, 512
+FLOPS = 2 * K * R * J + 2 * R * N * O
+
+F32 = mybir.dt.float32
+BF16 = mybir.dt.bfloat16
+I32 = mybir.dt.int32
+U32 = mybir.dt.uint32
+U16 = mybir.dt.uint16
+U8 = mybir.dt.uint8
+FP8X4 = mybir.dt.float8_e4m3fn_x4
+FP4X4 = mybir.dt.float4_e2m1fn_x4
+COPY = mybir.ActivationFunctionType.Copy
+ALU = mybir.AluOpType
+
+P = 128
+PACK = 4
+QUAD = 32
+
+
+def tile_picked_tokens_codes_one_boardmixed_respelled_plain_kernel(
+    tc, xt_words, xt_scales, ua, ha, sa, sb, va, ea, eb, offs, offs2, offs3, offs4, offs5, offs6, offs7, out
+):
+    nc = tc.nc
+    with ExitStack() as ctx:
+        lists = ctx.enter_context(tc.tile_pool(name="lists", bufs=1))
+        pool = ctx.enter_context(tc.tile_pool(name="pool", bufs=1))
+        psum = ctx.enter_context(tc.psum_pool(name="psum", bufs=1))
+
+        def load_list(name, src):
+            tile = lists.tile(list(src.shape), U16, name=name)
+            nc.sync.dma_start(tile[:], src)
+            return tile
+
+        def load_column(name, src, queue):
+            tile = pool.tile([P, PACK], F32, name=name)
+            queue.dma_start(tile[:], src.rearrange("(p t) o -> p (t o)", t=PACK))
+            return tile
+
+        def load_rows(name, src, t):
+            tile = pool.tile([P, src.shape[1]], F32, name=name, align_bytes=64)
+            nc.sync.dma_start(tile[:], src.rearrange("(p t) c -> t p c", t=PACK)[t])
+            return tile
+
+        list2 = load_list("list2", offs2)
+        ha_t = load_column("ha_t", ha, nc.scalar)
+        ea_t = load_column("ea_t", ea, nc.gpsimd)
+        eb_t = load_column("eb_t", eb, nc.gpsimd)
+        sa_t = load_column("sa_t", sa, nc.gpsimd)
+        sb_t = load_column("sb_t", sb, nc.gpsimd)
+        ua_t = [load_rows("ua%d" % t, ua, t) for t in range(2)]
+        list1 = load_list("list1", offs)
+        staged = pool.tile([PACK, PACK, T // 4], I32, name="staged")
+        nc.sync.dma_start(staged[:], xt_scales[0].bitcast(I32).rearrange("(q r) c -> r q c", r=PACK))
+        words = pool.tile([P, 2 * T], U8, name="words")
+        nc.sync.dma_start(words[:].bitcast(I32), xt_words[0].bitcast(I32))
+        ua_t.extend(load_rows("ua%d" % t, ua, t) for t in range(2, PACK))
+        list6 = load_list("list6", offs6)
+        va_t = [load_rows("va%d" % t, va, t) for t in range(2)]
+        list3 = load_list("list3", offs3)
+        va_t.extend(load_rows("va%d" % t, va, t) for t in range(2, PACK))
+        list7 = load_list("list7", offs7)
+        list4 = load_list("list4", offs4)
+        list5 = load_list("list5", offs5)
+
+        scales = pool.tile([P, T], U8, name="scales")
+        nc.vector.memset(scales[:].bitcast(I32), 0)
+        pw = [pool.tile([P, C], F32, name="pw%d" % t) for t in range(PACK)]
+        for t in range(PACK):
+            nc.vector.memset(pw[t][:], 0.0)
+
+        wc = pool.tile([P, PACK, R], BF16, name="wc")
+        wc_in = pool.tile([P, PACK, P, PACK], BF16, name="wc_in", align_bytes=64)
+        half = R // 2
+        for t in range(PACK - 1):
+            nc.scalar.activation(wc[:, t, :], ua_t[t][:].indirect(list2[:]), COPY, scale=ha_t[:, t : t + 1])
+        last = PACK - 1
+        for h in range(2):
+            nc.scalar.activation(
+                wc[:, last, h * half : (h + 1) * half],
+                ua_t[last][:].indirect(list2[:, h * half // 16 : (h + 1) * half // 16]),
+                COPY,
+                scale=ha_t[:, last : last + 1],
+            )
+
+        for q in range(PACK):
+            nc.vector.tensor_copy(scales[QUAD * q : QUAD * q + PACK, :].bitcast(I32), staged[:, q, :])
+        x_words = pool.tile([P, 2 * J], U8, name="x_words", align_bytes=64)
+        x_scales = pool.tile([P, J], U8, name="x_scales", align_bytes=64)
+        nc.vector.tensor_copy(x_scales[:], scales[:].indirect(list1[:]))
+        nc.vector.tensor_copy(x_words[:].bitcast(U16), words[:].bitcast(U16).indirect(list1[:]))
+
+        for h in range(2):
+            nc.vector.tensor_copy(
+                wc_in[:, :, h * P // 2 : (h + 1) * P // 2, :],
+                wc[:, :, h * half : (h + 1) * half].rearrange("p t (m u) -> p u m t", u=PACK),
+            )
+        wc_codes = pool.tile([P, R], U32, name="wc_codes", align_bytes=64)
+        wc_scales = pool.tile([P, R], U8, name="wc_scales", align_bytes=64)
+        a_ps = [psum.tile([P, J], F32, name="a_ps%d" % u) for u in range(2)]
+        a_late = psum.tile([P, 2, J], F32, name="a_late")
+        banks = [a_ps[0][:], a_ps[1][:], a_late[:, 0, :], a_late[:, 1, :]]
+        for u in range(PACK):
+            cols = slice(u * P, (u + 1) * P)
+            nc.vector.quantize_mx(
+                out=wc_codes[:, cols].bitcast(FP8X4),
+                scales=wc_scales[:, cols],
+                in_=wc_in[:, u].rearrange("p m t -> p (m t)"),
+            )
+            nc.tensor.matmul_mx(
+                out=banks[u],
+                lhsT=wc_codes[:, cols].bitcast(FP8X4),
+                lhsT_scale=wc_scales[:, cols],
+                rhs=x_words[:].bitcast(FP4X4),
+                rhs_scale=x_scales[:],
+                start=True,
+                stop=True,
+            )
+        for u in range(2):
+            a_sb = pool.tile([P, J], F32, name="a_sb%d" % u)
+            nc.vector.tensor_copy(a_sb[:], a_ps[u][:])
+            nc.vector.tensor_copy(pw[u][:].indirect(list3[:]), a_sb[:])
+
+        vc = pool.tile([P, PACK, N], BF16, name="vc")
+        vcd = [pool.tile([P, Z], F32, name="vcd%d" % t) for t in range(PACK)]
+        for t in range(PACK):
+            nc.scalar.activation(vcd[t][:], va_t[t][:].indirect(list6[:]), COPY, scale=ea_t[:, t : t + 1])
+        a_late_sb = pool.tile([P, 2, J], F32, name="a_late_sb", tag="va1", align_bytes=64)
+        nc.scalar.copy(a_late_sb[:], a_late[:])
+        for u in range(2):
+            nc.vector.tensor_copy(pw[2 + u][:].indirect(list3[:]), a_late_sb[:, u, :])
+        for t in range(PACK):
+            nc.scalar.activation(vc[:, t, :], vcd[t][:].indirect(list7[:]), COPY, scale=eb_t[:, t : t + 1])
+
+        read = pool.tile([P, 2, PACK, O], F32, name="read", tag="va3", align_bytes=64)
+        for t in range(PACK):
+            nc.scalar.activation(read[:, 0, t, :], pw[t][:].indirect(list4[:]), COPY, scale=sa_t[:, t : t + 1])
+            nc.scalar.activation(read[:, 1, t, :], pw[t][:].indirect(list5[:]), COPY, scale=sb_t[:, t : t + 1])
+
+        vc_in = pool.tile([P, 2, P, PACK], BF16, name="vc_in", tag="va1", align_bytes=64)
+        nc.vector.tensor_copy(vc_in[:], vc[:].rearrange("p t (m u) -> p u m t", u=2))
+        diff = pool.tile([P, PACK, O], F32, name="diff")
+        nc.vector.tensor_tensor(diff[:, :last, :], read[:, 0, :last, :], read[:, 1, :last, :], ALU.subtract)
+        vc_codes = pool.tile([P, N], U32, name="vc_codes", align_bytes=64)
+        vc_scales = pool.tile([P, N], U8, name="vc_scales", align_bytes=64)
+        nc.vector.quantize_mx(
+            out=vc_codes[:].bitcast(FP8X4), scales=vc_scales[:], in_=vc_in[:].rearrange("p u m t -> p (u m t)")
+        )
+        nc.vector.tensor_tensor(diff[:, last, :], read[:, 0, last, :], read[:, 1, last, :], ALU.subtract)
+        hid_in = pool.tile([P, O, PACK], BF16, name="hid_in", align_bytes=64)
+        by_place = diff[:].rearrange("p t o -> p o t")
+        nc.vector.scalar_tensor_tensor(hid_in[:], by_place, -1.0, by_place, ALU.mult, ALU.max)
+        hid_codes = pool.tile([P, O], U32, name="hid_codes", align_bytes=64)
+        hid_scales = pool.tile([P, O], U8, name="hid_scales", align_bytes=64)
+        nc.vector.quantize_mx(
+            out=hid_codes[:].bitcast(FP8X4), scales=hid_scales[:], in_=hid_in[:].rearrange("p o t -> p (o t)")
+        )
+
+        result = pool.tile([P, 2, O], F32, name="result")
+        for u in range(2):
+            cols = slice(u * P, (u + 1) * P)
+            bank = psum.tile([P, O], F32, name="y_ps%d" % u)
+            nc.tensor.matmul_mx(
+                out=bank[:],
+                lhsT=vc_codes[:, cols].bitcast(FP8X4),
+                lhsT_scale=vc_scales[:, cols],
+                rhs=hid_codes[:].bitcast(FP8X4),
+                rhs_scale=hid_scales[:],
+                start=True,
+                stop=True,
+            )
+            if u == 0:
+                nc.scalar.copy(result[:, u, :], bank[:])
+            else:
+                nc.vector.tensor_copy(result[:, u, :], bank[:])
+        nc.sync.dma_start(out.rearrange("(m u) o -> m u o", u=2), result[:])

@@ -66,6 +66,9 @@ def tile_picked_tokens_codes_one_boardmixed_respelled_plain_kernel(
         list4 = load_list("list4", offs4)
         list5 = load_list("list5", offs5)
 
+        warm = pool.tile([P, 16], F32, name="warm")
+        nc.vector.memset(warm[:, 0:8], 0.0)
+        nc.scalar.activation(warm[:, 8:9], warm[:, 0:1], COPY)
         scales = pool.tile([P, T], U8, name="scales")
         nc.vector.memset(scales[:].bitcast(I32), 0)
         pw = [pool.tile([P, C], F32, name="pw%d" % t) for t in range(PACK)]

@@ -14,6 +14,7 @@ U8 = mybir.dt.uint8
 FP8X4 = mybir.dt.float8_e4m3fn_x4
 FP4X4 = mybir.dt.float4_e2m1fn_x4
 COPY = mybir.ActivationFunctionType.Copy
+ABS = mybir.ActivationFunctionType.Abs
 ALU = mybir.AluOpType
 
 P = 128
@@ -53,11 +54,15 @@ def tile_picked_tokens_codes_one_boardmixed_respelled_plain_kernel(
         sb_t = load_column("sb_t", sb, nc.gpsimd)
         ua_t = [load_rows("ua%d" % t, ua, t) for t in range(2)]
         list1 = load_list("list1", offs)
-        staged = pool.tile([PACK, PACK, T // 4], I32, name="staged")
-        nc.sync.dma_start(staged[:], xt_scales[0].bitcast(I32).rearrange("(q r) c -> r q c", r=PACK))
+        scales = pool.tile([P, T], U8, name="scales")
+        nc.vector.memset(scales[:].bitcast(I32), 0)
+        for q in range(PACK):
+            nc.sync.dma_start(
+                scales[QUAD * q : QUAD * q + PACK, :].bitcast(I32), xt_scales[0, PACK * q : PACK * (q + 1), :].bitcast(I32)
+            )
+        ua_t.extend(load_rows("ua%d" % t, ua, t) for t in range(2, PACK))
         words = pool.tile([P, 2 * T], U8, name="words")
         nc.sync.dma_start(words[:].bitcast(I32), xt_words[0].bitcast(I32))
-        ua_t.extend(load_rows("ua%d" % t, ua, t) for t in range(2, PACK))
         list6 = load_list("list6", offs6)
         va_t = [load_rows("va%d" % t, va, t) for t in range(2)]
         list3 = load_list("list3", offs3)
@@ -69,8 +74,6 @@ def tile_picked_tokens_codes_one_boardmixed_respelled_plain_kernel(
         warm = pool.tile([P, 16], F32, name="warm")
         nc.vector.memset(warm[:, 0:8], 0.0)
         nc.scalar.activation(warm[:, 8:9], warm[:, 0:1], COPY)
-        scales = pool.tile([P, T], U8, name="scales")
-        nc.vector.memset(scales[:].bitcast(I32), 0)
         pw = [pool.tile([P, C], F32, name="pw%d" % t) for t in range(PACK)]
         for t in range(PACK):
             nc.vector.memset(pw[t][:], 0.0)
@@ -89,23 +92,19 @@ def tile_picked_tokens_codes_one_boardmixed_respelled_plain_kernel(
                 scale=ha_t[:, last : last + 1],
             )
 
-        for q in range(PACK):
-            nc.vector.tensor_copy(scales[QUAD * q : QUAD * q + PACK, :].bitcast(I32), staged[:, q, :])
         x_words = pool.tile([P, 2 * J], U8, name="x_words", align_bytes=64)
         x_scales = pool.tile([P, J], U8, name="x_scales", align_bytes=64)
         nc.vector.tensor_copy(x_scales[:], scales[:].indirect(list1[:]))
         nc.vector.tensor_copy(x_words[:].bitcast(U16), words[:].bitcast(U16).indirect(list1[:]))
 
-        for h in range(2):
-            nc.vector.tensor_copy(
-                wc_in[:, :, h * P // 2 : (h + 1) * P // 2, :],
-                wc[:, :, h * half : (h + 1) * half].rearrange("p t (m u) -> p u m t", u=PACK),
-            )
+        dealt = wc[:].rearrange("p t (m u) -> p u m t", u=PACK)
+        nc.vector.tensor_copy(wc_in[:, :, : P // 2, :], dealt[:, :, : P // 2, :])
+        for pair in range(2):
+            tiles = slice(2 * pair, 2 * pair + 2)
+            nc.vector.tensor_copy(wc_in[:, tiles, P // 2 :, :], dealt[:, tiles, P // 2 :, :])
         wc_codes = pool.tile([P, R], U32, name="wc_codes", align_bytes=64)
         wc_scales = pool.tile([P, R], U8, name="wc_scales", align_bytes=64)
-        a_ps = [psum.tile([P, J], F32, name="a_ps%d" % u) for u in range(2)]
-        a_late = psum.tile([P, 2, J], F32, name="a_late")
-        banks = [a_ps[0][:], a_ps[1][:], a_late[:, 0, :], a_late[:, 1, :]]
+        a_ps = [psum.tile([P, J], F32, name="a_ps%d" % u) for u in range(PACK)]
         for u in range(PACK):
             cols = slice(u * P, (u + 1) * P)
             nc.vector.quantize_mx(
@@ -114,7 +113,7 @@ def tile_picked_tokens_codes_one_boardmixed_respelled_plain_kernel(
                 in_=wc_in[:, u].rearrange("p m t -> p (m t)"),
             )
             nc.tensor.matmul_mx(
-                out=banks[u],
+                out=a_ps[u][:],
                 lhsT=wc_codes[:, cols].bitcast(FP8X4),
                 lhsT_scale=wc_scales[:, cols],
                 rhs=x_words[:].bitcast(FP4X4),
@@ -122,8 +121,8 @@ def tile_picked_tokens_codes_one_boardmixed_respelled_plain_kernel(
                 start=True,
                 stop=True,
             )
-        for u in range(2):
-            a_sb = pool.tile([P, J], F32, name="a_sb%d" % u)
+        for u in range(PACK):
+            a_sb = pool.tile([P, J], F32, name="a_sb%d" % u, align_bytes=64)
             nc.vector.tensor_copy(a_sb[:], a_ps[u][:])
             nc.vector.tensor_copy(pw[u][:].indirect(list3[:]), a_sb[:])
 
@@ -131,10 +130,6 @@ def tile_picked_tokens_codes_one_boardmixed_respelled_plain_kernel(
         vcd = [pool.tile([P, Z], F32, name="vcd%d" % t) for t in range(PACK)]
         for t in range(PACK):
             nc.scalar.activation(vcd[t][:], va_t[t][:].indirect(list6[:]), COPY, scale=ea_t[:, t : t + 1])
-        a_late_sb = pool.tile([P, 2, J], F32, name="a_late_sb", tag="va1", align_bytes=64)
-        nc.scalar.copy(a_late_sb[:], a_late[:])
-        for u in range(2):
-            nc.vector.tensor_copy(pw[2 + u][:].indirect(list3[:]), a_late_sb[:, u, :])
         for t in range(PACK):
             nc.scalar.activation(vc[:, t, :], vcd[t][:].indirect(list7[:]), COPY, scale=eb_t[:, t : t + 1])
 
@@ -143,19 +138,18 @@ def tile_picked_tokens_codes_one_boardmixed_respelled_plain_kernel(
             nc.scalar.activation(read[:, 0, t, :], pw[t][:].indirect(list4[:]), COPY, scale=sa_t[:, t : t + 1])
             nc.scalar.activation(read[:, 1, t, :], pw[t][:].indirect(list5[:]), COPY, scale=sb_t[:, t : t + 1])
 
-        vc_in = pool.tile([P, 2, P, PACK], BF16, name="vc_in", tag="va1", align_bytes=64)
+        vc_in = pool.tile([P, 2, P, PACK], BF16, name="vc_in", tag="a_sb3", align_bytes=64)
         nc.vector.tensor_copy(vc_in[:], vc[:].rearrange("p t (m u) -> p u m t", u=2))
         diff = pool.tile([P, PACK, O], F32, name="diff")
         nc.vector.tensor_tensor(diff[:, :last, :], read[:, 0, :last, :], read[:, 1, :last, :], ALU.subtract)
+        nc.vector.tensor_tensor(diff[:, last, :], read[:, 0, last, :], read[:, 1, last, :], ALU.subtract)
         vc_codes = pool.tile([P, N], U32, name="vc_codes", align_bytes=64)
         vc_scales = pool.tile([P, N], U8, name="vc_scales", align_bytes=64)
         nc.vector.quantize_mx(
             out=vc_codes[:].bitcast(FP8X4), scales=vc_scales[:], in_=vc_in[:].rearrange("p u m t -> p (u m t)")
         )
-        nc.vector.tensor_tensor(diff[:, last, :], read[:, 0, last, :], read[:, 1, last, :], ALU.subtract)
         hid_in = pool.tile([P, O, PACK], BF16, name="hid_in", align_bytes=64)
-        by_place = diff[:].rearrange("p t o -> p o t")
-        nc.vector.scalar_tensor_tensor(hid_in[:], by_place, -1.0, by_place, ALU.mult, ALU.max)
+        nc.scalar.activation(hid_in[:], diff[:].rearrange("p t o -> p o t"), ABS)
         hid_codes = pool.tile([P, O], U32, name="hid_codes", align_bytes=64)
         hid_scales = pool.tile([P, O], U8, name="hid_scales", align_bytes=64)
         nc.vector.quantize_mx(

@@ -42,7 +42,7 @@ def tile_picked_tokens_codes_one_boardmixed_respelled_plain_kernel(
             return tile
 
         def load_rows(name, src, t):
-            tile = pool.tile([P, src.shape[1]], F32, name=name, align_bytes=64)
+            tile = pool.tile([P, src.shape[1]], F32, name=name)
             nc.sync.dma_start(tile[:], src.rearrange("(p t) c -> t p c", t=PACK)[t])
             return tile
 
@@ -122,7 +122,7 @@ def tile_picked_tokens_codes_one_boardmixed_respelled_plain_kernel(
                 stop=True,
             )
         for u in range(PACK):
-            a_sb = pool.tile([P, J], F32, name="a_sb%d" % u, align_bytes=64)
+            a_sb = pool.tile([P, J], F32, name="a_sb%d" % u)
             nc.vector.tensor_copy(a_sb[:], a_ps[u][:])
             nc.vector.tensor_copy(pw[u][:].indirect(list3[:]), a_sb[:])
 
@@ -130,26 +130,40 @@ def tile_picked_tokens_codes_one_boardmixed_respelled_plain_kernel(
         vcd = [pool.tile([P, Z], F32, name="vcd%d" % t) for t in range(PACK)]
         for t in range(PACK):
             nc.scalar.activation(vcd[t][:], va_t[t][:].indirect(list6[:]), COPY, scale=ea_t[:, t : t + 1])
-        for t in range(PACK):
+        for t in range(last):
             nc.scalar.activation(vc[:, t, :], vcd[t][:].indirect(list7[:]), COPY, scale=eb_t[:, t : t + 1])
 
-        read = pool.tile([P, 2, PACK, O], F32, name="read", tag="va3", align_bytes=64)
+        read = pool.tile([P, 2, PACK, O], F32, name="read", tag="vcd1")
         for t in range(PACK):
             nc.scalar.activation(read[:, 0, t, :], pw[t][:].indirect(list4[:]), COPY, scale=sa_t[:, t : t + 1])
             nc.scalar.activation(read[:, 1, t, :], pw[t][:].indirect(list5[:]), COPY, scale=sb_t[:, t : t + 1])
 
-        vc_in = pool.tile([P, 2, P, PACK], BF16, name="vc_in", tag="a_sb3", align_bytes=64)
-        nc.vector.tensor_copy(vc_in[:], vc[:].rearrange("p t (m u) -> p u m t", u=2))
+        for u in range(2):
+            nc.scalar.activation(
+                vc[:, last, u * P : (u + 1) * P],
+                vcd[last][:].indirect(list7[:, u * P // 16 : (u + 1) * P // 16]),
+                COPY,
+                scale=eb_t[:, last : last + 1],
+            )
+
         diff = pool.tile([P, PACK, O], F32, name="diff")
         nc.vector.tensor_tensor(diff[:, :last, :], read[:, 0, :last, :], read[:, 1, :last, :], ALU.subtract)
         nc.vector.tensor_tensor(diff[:, last, :], read[:, 0, last, :], read[:, 1, last, :], ALU.subtract)
-        vc_codes = pool.tile([P, N], U32, name="vc_codes", align_bytes=64)
-        vc_scales = pool.tile([P, N], U8, name="vc_scales", align_bytes=64)
-        nc.vector.quantize_mx(
-            out=vc_codes[:].bitcast(FP8X4), scales=vc_scales[:], in_=vc_in[:].rearrange("p u m t -> p (u m t)")
-        )
         hid_in = pool.tile([P, O, PACK], BF16, name="hid_in", align_bytes=64)
         nc.scalar.activation(hid_in[:], diff[:].rearrange("p t o -> p o t"), ABS)
+
+        vc_in = pool.tile([P, 2, P, PACK], BF16, name="vc_in", align_bytes=64)
+        vc_codes = pool.tile([P, N], U32, name="vc_codes", align_bytes=64)
+        vc_scales = pool.tile([P, N], U8, name="vc_scales", align_bytes=64)
+        for u in range(2):
+            nc.vector.tensor_copy(vc_in[:, u], vc[:, :, u * P : (u + 1) * P].rearrange("p t m -> p m t"))
+        for u in range(2):
+            cols = slice(u * P, (u + 1) * P)
+            nc.vector.quantize_mx(
+                out=vc_codes[:, cols].bitcast(FP8X4),
+                scales=vc_scales[:, cols],
+                in_=vc_in[:, u].rearrange("p m t -> p (m t)"),
+            )
         hid_codes = pool.tile([P, O], U32, name="hid_codes", align_bytes=64)
         hid_scales = pool.tile([P, O], U8, name="hid_scales", align_bytes=64)
         nc.vector.quantize_mx(
@@ -170,7 +184,8 @@ def tile_picked_tokens_codes_one_boardmixed_respelled_plain_kernel(
                 stop=True,
             )
             if u == 0:
-                nc.scalar.copy(result[:, u, :], bank[:])
-            else:
                 nc.vector.tensor_copy(result[:, u, :], bank[:])
-        nc.sync.dma_start(out.rearrange("(m u) o -> m u o", u=2), result[:])
+                nc.sync.dma_start(out[cols, :], result[:, u, :])
+            else:
+                nc.scalar.copy(result[:, u, :], bank[:])
+                nc.scalar.dma_start(out[cols, :], result[:, u, :])

from contextlib import ExitStack

import concourse.mybir as mybir

K, J, R, T, F, C, O, N, S, Z = 512, 256, 512, 1024, 1024, 512, 128, 256, 1024, 512
FLOPS = 2 * K * R * J + 2 * R * N * O

F32 = mybir.dt.float32
BF16 = mybir.dt.bfloat16
I32 = mybir.dt.int32
U32 = mybir.dt.uint32
U16 = mybir.dt.uint16
U8 = mybir.dt.uint8
FP8X4 = mybir.dt.float8_e4m3fn_x4
FP4X4 = mybir.dt.float4_e2m1fn_x4
COPY = mybir.ActivationFunctionType.Copy
ABS = mybir.ActivationFunctionType.Abs
ALU = mybir.AluOpType

P = 128
PACK = 4
QUAD = 32


def tile_picked_tokens_codes_one_boardmixed_respelled_plain_kernel(
    tc, xt_words, xt_scales, ua, ha, sa, sb, va, ea, eb, offs, offs2, offs3, offs4, offs5, offs6, offs7, out
):
    nc = tc.nc
    with ExitStack() as ctx:
        lists = ctx.enter_context(tc.tile_pool(name="lists", bufs=1))
        pool = ctx.enter_context(tc.tile_pool(name="pool", bufs=1))
        psum = ctx.enter_context(tc.psum_pool(name="psum", bufs=1))

        def load_list(name, src):
            tile = lists.tile(list(src.shape), U16, name=name)
            nc.sync.dma_start(tile[:], src)
            return tile

        def load_column(name, src, queue):
            tile = pool.tile([P, PACK], F32, name=name)
            queue.dma_start(tile[:], src.rearrange("(p t) o -> p (t o)", t=PACK))
            return tile

        def load_rows(name, src, t):
            tile = pool.tile([P, src.shape[1]], F32, name=name)
            nc.sync.dma_start(tile[:], src.rearrange("(p t) c -> t p c", t=PACK)[t])
            return tile

        list2 = load_list("list2", offs2)
        ha_t = load_column("ha_t", ha, nc.scalar)
        ea_t = load_column("ea_t", ea, nc.gpsimd)
        eb_t = load_column("eb_t", eb, nc.gpsimd)
        sa_t = load_column("sa_t", sa, nc.gpsimd)
        sb_t = load_column("sb_t", sb, nc.gpsimd)
        ua_t = [load_rows("ua%d" % t, ua, t) for t in range(2)]
        list1 = load_list("list1", offs)
        scales = pool.tile([P, T], U8, name="scales")
        nc.vector.memset(scales[:].bitcast(I32), 0)
        for q in range(PACK):
            nc.sync.dma_start(
                scales[QUAD * q : QUAD * q + PACK, :].bitcast(I32), xt_scales[0, PACK * q : PACK * (q + 1), :].bitcast(I32)
            )
        ua_t.extend(load_rows("ua%d" % t, ua, t) for t in range(2, PACK))
        words = pool.tile([P, 2 * T], U8, name="words")
        nc.sync.dma_start(words[:].bitcast(I32), xt_words[0].bitcast(I32))
        list6 = load_list("list6", offs6)
        va_t = [load_rows("va%d" % t, va, t) for t in range(2)]
        list3 = load_list("list3", offs3)
        va_t.extend(load_rows("va%d" % t, va, t) for t in range(2, PACK))
        list7 = load_list("list7", offs7)
        list4 = load_list("list4", offs4)
        list5 = load_list("list5", offs5)

        warm = pool.tile([P, 16], F32, name="warm")
        nc.vector.memset(warm[:, 0:8], 0.0)
        nc.scalar.activation(warm[:, 8:9], warm[:, 0:1], COPY)
        pw = [pool.tile([P, C], F32, name="pw%d" % t) for t in range(PACK)]
        for t in range(PACK):
            nc.vector.memset(pw[t][:], 0.0)

        wc = pool.tile([P, PACK, R], BF16, name="wc")
        wc_in = pool.tile([P, PACK, P, PACK], BF16, name="wc_in", align_bytes=64)
        half = R // 2
        for t in range(PACK - 1):
            nc.scalar.activation(wc[:, t, :], ua_t[t][:].indirect(list2[:]), COPY, scale=ha_t[:, t : t + 1])
        last = PACK - 1
        for h in range(2):
            nc.scalar.activation(
                wc[:, last, h * half : (h + 1) * half],
                ua_t[last][:].indirect(list2[:, h * half // 16 : (h + 1) * half // 16]),
                COPY,
                scale=ha_t[:, last : last + 1],
            )

        x_words = pool.tile([P, 2 * J], U8, name="x_words", align_bytes=64)
        x_scales = pool.tile([P, J], U8, name="x_scales", align_bytes=64)
        nc.vector.tensor_copy(x_scales[:], scales[:].indirect(list1[:]))
        nc.vector.tensor_copy(x_words[:].bitcast(U16), words[:].bitcast(U16).indirect(list1[:]))

        dealt = wc[:].rearrange("p t (m u) -> p u m t", u=PACK)
        nc.vector.tensor_copy(wc_in[:, :, : P // 2, :], dealt[:, :, : P // 2, :])
        for pair in range(2):
            tiles = slice(2 * pair, 2 * pair + 2)
            nc.vector.tensor_copy(wc_in[:, tiles, P // 2 :, :], dealt[:, tiles, P // 2 :, :])
        wc_codes = pool.tile([P, R], U32, name="wc_codes", align_bytes=64)
        wc_scales = pool.tile([P, R], U8, name="wc_scales", align_bytes=64)
        a_ps = [psum.tile([P, J], F32, name="a_ps%d" % u) for u in range(PACK)]
        for u in range(PACK):
            cols = slice(u * P, (u + 1) * P)
            nc.vector.quantize_mx(
                out=wc_codes[:, cols].bitcast(FP8X4),
                scales=wc_scales[:, cols],
                in_=wc_in[:, u].rearrange("p m t -> p (m t)"),
            )
            nc.tensor.matmul_mx(
                out=a_ps[u][:],
                lhsT=wc_codes[:, cols].bitcast(FP8X4),
                lhsT_scale=wc_scales[:, cols],
                rhs=x_words[:].bitcast(FP4X4),
                rhs_scale=x_scales[:],
                start=True,
                stop=True,
            )
        for u in range(PACK):
            a_sb = pool.tile([P, J], F32, name="a_sb%d" % u)
            nc.vector.tensor_copy(a_sb[:], a_ps[u][:])
            nc.vector.tensor_copy(pw[u][:].indirect(list3[:]), a_sb[:])

        vc = pool.tile([P, PACK, N], BF16, name="vc")
        vcd = [pool.tile([P, Z], F32, name="vcd%d" % t) for t in range(PACK)]
        for t in range(PACK):
            nc.scalar.activation(vcd[t][:], va_t[t][:].indirect(list6[:]), COPY, scale=ea_t[:, t : t + 1])
        for t in range(last):
            nc.scalar.activation(vc[:, t, :], vcd[t][:].indirect(list7[:]), COPY, scale=eb_t[:, t : t + 1])

        read = pool.tile([P, 2, PACK, O], F32, name="read", tag="vcd1")
        for t in range(PACK):
            nc.scalar.activation(read[:, 0, t, :], pw[t][:].indirect(list4[:]), COPY, scale=sa_t[:, t : t + 1])
            nc.scalar.activation(read[:, 1, t, :], pw[t][:].indirect(list5[:]), COPY, scale=sb_t[:, t : t + 1])

        for u in range(2):
            nc.scalar.activation(
                vc[:, last, u * P : (u + 1) * P],
                vcd[last][:].indirect(list7[:, u * P // 16 : (u + 1) * P // 16]),
                COPY,
                scale=eb_t[:, last : last + 1],
            )

        diff = pool.tile([P, PACK, O], F32, name="diff")
        nc.vector.tensor_tensor(diff[:, :last, :], read[:, 0, :last, :], read[:, 1, :last, :], ALU.subtract)
        nc.vector.tensor_tensor(diff[:, last, :], read[:, 0, last, :], read[:, 1, last, :], ALU.subtract)
        hid_in = pool.tile([P, O, PACK], BF16, name="hid_in", align_bytes=64)
        nc.scalar.activation(hid_in[:], diff[:].rearrange("p t o -> p o t"), ABS)

        vc_in = pool.tile([P, 2, P, PACK], BF16, name="vc_in", align_bytes=64)
        vc_codes = pool.tile([P, N], U32, name="vc_codes", align_bytes=64)
        vc_scales = pool.tile([P, N], U8, name="vc_scales", align_bytes=64)
        for u in range(2):
            nc.vector.tensor_copy(vc_in[:, u], vc[:, :, u * P : (u + 1) * P].rearrange("p t m -> p m t"))
        for u in range(2):
            cols = slice(u * P, (u + 1) * P)
            nc.vector.quantize_mx(
                out=vc_codes[:, cols].bitcast(FP8X4),
                scales=vc_scales[:, cols],
                in_=vc_in[:, u].rearrange("p m t -> p (m t)"),
            )
        hid_codes = pool.tile([P, O], U32, name="hid_codes", align_bytes=64)
        hid_scales = pool.tile([P, O], U8, name="hid_scales", align_bytes=64)
        nc.vector.quantize_mx(
            out=hid_codes[:].bitcast(FP8X4), scales=hid_scales[:], in_=hid_in[:].rearrange("p o t -> p (o t)")
        )

        result = pool.tile([P, 2, O], F32, name="result")
        for u in range(2):
            cols = slice(u * P, (u + 1) * P)
            bank = psum.tile([P, O], F32, name="y_ps%d" % u)
            nc.tensor.matmul_mx(
                out=bank[:],
                lhsT=vc_codes[:, cols].bitcast(FP8X4),
                lhsT_scale=vc_scales[:, cols],
                rhs=hid_codes[:].bitcast(FP8X4),
                rhs_scale=hid_scales[:],
                start=True,
                stop=True,
            )
            if u == 0:
                nc.vector.tensor_copy(result[:, u, :], bank[:])
                nc.sync.dma_start(out[cols, :], result[:, u, :])
            else:
                nc.scalar.copy(result[:, u, :], bank[:])
                nc.scalar.dma_start(out[cols, :], result[:, u, :])
